import numpy as np, ml_dtypes
CORES = [5,29,101,125,133,157,229,253]
N = 8
import mx_ref
BF = ml_dtypes.bfloat16
def entries(a):
    return np.ascontiguousarray(a.T).reshape(-1)
def table(e):
    return np.ascontiguousarray(np.reshape(e, (-1, 16)).T).astype(np.int32)
def cut(t, i, w=512):
    return t[:, w * i:w * i + w]
def decode(q):
    o = []
    for b in range(4):
        e = np.zeros((128, 128, 4), np.float32); e[np.arange(128), np.arange(128), b] = 1
        o.append(mx_ref.matmul(mx_ref.quantize(e.reshape(128, 512).astype(BF)), q))
    return np.stack(o, axis=2).reshape(128, -1)
def f(rng, *shape):
    return mx_ref.flush((rng.standard_normal(shape, dtype=np.float32) * np.exp2(rng.integers(-2, 3, shape[:-1] + (1,)))).astype(BF))
def wide(rng, *shape, cols=0):
    v = rng.standard_normal(shape, dtype=np.float32) * np.exp2(rng.integers(-12, 13, shape)).astype(np.float32)
    if cols: v *= np.repeat(np.exp2(rng.integers(-cols, cols + 1, shape[:-2] + (1, shape[-1] // 4))) * (rng.random(shape[:-2] + (1, shape[-1] // 4)) > 0.0625), 4, axis=-1).astype(np.float32)
    return mx_ref.flush(v.astype(BF))
T, K, O = 256, 256, 1
HA = (1237, 1811, 947, 1543, 2017, 733, 1409, 1699)
HB = (40503, 12289, 58111, 3571, 27644, 61007, 19211, 50021)
def setup_inputs(rng):
    return {"tb": f(rng, N, 128, 4 * K), "ids": np.stack([table(rng.integers(0, 4096, T)) for r in range(N)]), "w": f(rng, N, 128, 512 * O)}
def setup_inputs_alike(rng):
    d = setup_inputs(rng); e = rng.integers(0, 4096, T)
    d["ids"] = np.stack([table(e) for r in range(N)]); return d
def setup_inputs_ends(rng):
    d = setup_inputs(rng); o = []
    for r in range(N):
        e = rng.choice([0, 4095], T); e[rng.permutation(T)[:2]] = [0, 4095]
        o.append(table(e))
    d["ids"] = np.stack(o); return d
def setup_inputs_order(rng):
    d = setup_inputs(rng); t = rng.standard_normal((N, 128, 4 * K), dtype=np.float32)
    one = rng.permutation(np.concatenate([np.arange(N), rng.integers(0, N, 16 - N)]))
    for g in range(16):
        p = int(one[g]); o = int(rng.choice([q for q in range(N) if abs(q - p) >= 2]))
        size = np.float32(2.0 ** int(rng.integers(0, 3)))
        X = np.tile(rng.choice([-1, 1], (8, 4)).astype(np.float32) * size, (1, K))
        v = t[:, 8 * g:8 * g + 8]; v *= size * np.float32(2.0 ** -14)
        v[min(p, o)] = X; v[max(p, o)] = -X
    d["tb"] = mx_ref.flush(t.astype(BF)); return d
def setup_inputs_same(rng):
    d = setup_inputs(rng)
    d["ids"] = np.stack([table(np.full(T, rng.integers(0, 4096))) for r in range(N)]); return d
def setup_inputs_spread(rng):
    d = setup_inputs(rng); d["tb"] = wide(rng, N, 128, 4 * K, cols=8); return d
def check_inputs(d):
    b = []
    for r in range(N):
        e = entries(d["ids"][r])
        if e.min() < 0 or e.max() > 4095: b.append("ids")
    return b
def address(q, e):
    return ((e * HA[q] + HB[q]) >> 5) & (K - 1)
def reference(tb, ids, w):
    d = [decode(mx_ref.quantize(tb[q])).reshape(128, -1, 4) for q in range(N)]
    y = np.zeros((N, 128, O * T), np.float32)
    for r in range(N):
        e = entries(ids[r])
        v = d[0][:, address(0, e)]
        for q in range(1, N): v = v + d[q][:, address(q, e)]
        V = mx_ref.quantize(np.ascontiguousarray(v.reshape(128, -1)).astype(BF))
        for o in range(O): y[r][:, T * o:T * o + T] = mx_ref.matmul(mx_ref.quantize(np.ascontiguousarray(cut(w[r], o))), V)
    return {"y": y}

@@ -1,0 +1,314 @@
+from concourse.bass import DstId, RemoteDMATransfer
+from concourse.mybir import dt, AluOpType, ActivationFunctionType
+
+N, TOK, K = 8, 256, 256
+HA = (1237, 1811, 947, 1543, 2017, 733, 1409, 1699)
+HB = (40503, 12289, 58111, 3571, 27644, 61007, 19211, 50021)
+HT = TOK // 2
+L = HT // 16
+W = 4 * L
+
+SCRATCH = {
+    "codes": ("sbuf", [128, N * K], "float8_e4m3fn_x4"),
+    "planes": ("sbuf", [128, N * K], "uint8"),
+    "tt": ("sbuf", [128, 4 * K], "bfloat16"),
+    "wt": ("sbuf", [128, 512], "bfloat16"),
+    "wc": ("sbuf", [128, 128], "float8_e4m3fn_x4"),
+    "wp": ("sbuf", [128, 128], "uint8"),
+    "ones": ("sbuf", [128, 516], "bfloat16"),
+    "hot": ("sbuf", [128, 516], "bfloat16"),
+    "ec": ("sbuf", [128, 512], "float8_e4m3fn_x4"),
+    "ep": ("sbuf", [128, 512], "uint8"),
+    "ido": ("dram", [128, TOK // 128], "int32"),
+    "idd": ("dram", [128, TOK // 128], "int32"),
+    "idl": ("sbuf", [128, TOK // 16], "int32"),
+    "id4": ("sbuf", [128, W], "int32"),
+    "hx": ("sbuf", [128, N * W], "int32"),
+    "hc": ("sbuf", [128, N * W], "int32"),
+    "cst": ("sbuf", [128, N * W], "int32"),
+    "ofs": ("sbuf", [128, N * W], "int32"),
+    "off": ("sbuf", [128, N * W], "uint16"),
+    "dd": ("sbuf", [128, N * 4 * K], "bfloat16"),
+    "acc": ("sbuf", [128, 4 * HT], "float32"),
+    "vt": ("sbuf", [128, 4 * HT], "bfloat16"),
+    "vc": ("sbuf", [128, TOK], "float8_e4m3fn_x4"),
+    "vp": ("sbuf", [128, TOK], "uint8"),
+    "yt": ("sbuf", [128, TOK], "float32"),
+    "ps": ("psum", [128, 8 * 512], "float32"),
+}
+SEMAPHORES = (["s_tb", "s_ido", "s_ids", "s_w", "s_ones", "s_hot", "s_cst", "s_qt", "s_qe", "s_id4", "s_hx", "s_hc", "s_ofs", "s_off",
+               "s_qw", "s_o0", "s_o1", "r_ids", "r_codes", "r_plane", "r_sent", "r_v", "lv", "qv", "ym0", "ym1", "yc0", "yc1"]
+              + ["ac%d" % q for q in range(N)] + ["ap%d" % q for q in range(N)] + ["add%d" % k for k in range(N)]
+              + ["fp%d" % i for i in range(3)] + ["fc%d" % i for i in range(5)] + ["cu%d" % q for q in range(N)]
+              + ["mm%d_%d" % (q, b) for q in range(N) for b in range(4)])
+
+
+def planes_of(T, topo):
+    a = [q for q in range(N) if q == 0 or topo.same_plane(T.cores[0], T.cores[q])]
+    return a, [q for q in range(N) if q not in a]
+
+
+def sides(rank, T, topo):
+    a, b = planes_of(T, topo)
+    return (a, b) if rank in a else (b, a)
+
+
+def relays_of(rank, T, topo):
+    home = T.cores[rank]
+    mine, other = sides(rank, T, topo)
+    owners = [x for x in topo.cores_of(home) if x != home and all(topo.may_write(x, T.cores[d]) for d in other)]
+    near = [x for x in owners if topo.die(x) == topo.die(home)]
+    far = [x for x in owners if topo.die(x) != topo.die(home)]
+    return near[0], far[0]
+
+
+def helper(rank, T, topo):
+    return relays_of(rank, T, topo)[0]
+
+
+def direct(rank, T, topo):
+    mine, other = sides(rank, T, topo)
+    me = mine.index(rank)
+    return [helper(mine[me ^ x], T, topo) for x in (1, 2, 3)]
+
+
+def relayed(rank, T, topo):
+    mine, other = sides(rank, T, topo)
+    me = mine.index(rank)
+    return [[helper(other[me ^ x], T, topo) for x in xs] for xs in ((0, 1), (2, 3))]
+
+
+def count(m):
+    return bin(m).count("1")
+
+
+def common(src, dsts, topo):
+    m = topo.mask(src, dsts[0])
+    for d in dsts:
+        m &= topo.mask(src, d)
+    return m
+
+
+def copy_to(g, src, dsts, out, in_, remote_sem, local_sem, topo):
+    m = common(src, dsts, topo)
+    ids = []
+    for d in dsts:
+        rid, pid = topo.addr(d, src)
+        ids.append(DstId(rid=rid, pnc=pid))
+    g.remote_dma_fused([RemoteDMATransfer(dst_ids=ids, dma_engine_mask=m, remote_sem=remote_sem,
+                                          srcs=[in_], dsts=[out] * len(dsts))], local_sem=local_sem)
+    return count(m)
+
+
+def slot_of(q, T, topo):
+    a, b = planes_of(T, topo)
+    return (a + b).index(q)
+
+
+def slots(T, s, n):
+    return T.codes[:, K * s:K * s + K * n], T.planes[:, K * s:K * s + K * n]
+
+
+def relay(g, core, rank, dsts, T, topo):
+    S = T.sem
+    c, p = slots(T, slot_of(rank, T, topo), 1)
+    n = count(topo.mask(T.cores[rank], core))
+    g.wait_ge(S.r_plane, n)
+    sent = copy_to(g, core, dsts, p, p, S["ap%d" % rank], S.r_sent, topo)
+    g.wait_ge(S.r_codes, n)
+    return sent + copy_to(g, core, dsts, c.bitcast(dt.uint8), c.bitcast(dt.uint8), S["ac%d" % rank], S.r_sent, topo)
+
+
+def rank_program(g, core, T, topo):
+    rank = T.rank_of(core)
+    if rank is not None:
+        lookup_core(g, core, rank, True, T, topo)
+        return
+    for q, home in enumerate(T.cores):
+        if core in topo.cores_of(home):
+            H, F = relays_of(q, T, topo)
+            if core == H:
+                lookup_core(g, core, q, False, T, topo)
+            elif core == F:
+                sent = relay(g, core, q, relayed(q, T, topo)[1], T, topo)
+                g.wait_ge(T.sem.r_sent, sent)
+
+
+def lookup_core(g, core, rank, is_rank, T, topo):
+    S = T.sem
+    v = g.vector
+    home = T.cores[rank]
+    H, F = relays_of(rank, T, topo)
+    mine, other = sides(rank, T, topo)
+    me = mine.index(rank)
+    o = 2 - 2 * (me // 2)
+    n16 = count(topo.mask(H, home))
+
+    need = {}
+    for q in range(N):
+        if q == rank:
+            continue
+        for src, dsts in [(T.cores[q], direct(q, T, topo))] + list(zip(relays_of(q, T, topo), relayed(q, T, topo))):
+            if core in dsts:
+                need[q] = count(common(src, dsts, topo))
+
+    seq = list(range(N))
+    if seq[1] in mine:
+        seq[0], seq[1] = seq[1], seq[0]
+    order = [rank]
+    order += [q for q in seq if q in mine and q not in order][:1]
+    order += [q for q in seq if q not in order]
+    fplane = [[mine[me ^ 1]], mine[o:o + 2], other]
+    fcodes = [[mine[me ^ 1]], mine[o:o + 2], other[0:1], other[1:2], other[2:4]]
+    fcodes.sort(key=lambda qs: min(order.index(q) for q in qs))
+
+    if is_rank:
+        g.sync.dma_start(T.tt[:], T.tb[:]).then_inc(S.s_tb, 16)
+        g.scalar.dma_start(T.ido[:], T.ids[:]).then_inc(S.s_ido, 16)
+    else:
+        for eng in (g.sync, g.scalar):
+            eng.wait_ge(S.r_ids, n16)
+    for k in range(8):
+        eng = g.scalar if k % 2 == 0 else g.sync
+        eng.dma_start(T.idl[16 * k:16 * k + 16, :], T.ids[:] if is_rank else T.idd[:]).then_inc(S.s_ids, 16)
+    if is_rank:
+        g.sync.dma_start(T.wt[:], T.w[:]).then_inc(S.s_w, 16)
+
+    def part_starts():
+        g.iota(T.cst[:], [[0, N], [K, 4], [0, L]], 0, 0).then_inc(S.s_cst, 1)
+
+    def send(dsts, ap, sem):
+        return copy_to(g, core, dsts, ap, ap, sem, S.r_sent, topo)
+
+    g.wait_ge(S.s_ones, 1)
+    g.affine_select(T.hot[:], T.ones[:], [[-1, 516]], AluOpType.is_equal, 0.0, 3, 4).then_inc(S.s_hot, 1)
+    c, p = slots(T, slot_of(rank, T, topo), 1)
+    cb = c.bitcast(dt.uint8)
+    if is_rank:
+        ds = direct(rank, T, topo)
+        g.wait_ge(S.s_ido, 16)
+        sent = copy_to(g, core, [H], T.idd[:], T.ido[:], S.r_ids, S.r_sent, topo)
+        g.wait_ge(S.s_qt, 1)
+        sent += send([H, F], p, S.r_plane)
+        sent += send([H, F], cb, S.r_codes)
+        sent += send(ds, p, S["ap%d" % rank])
+        sent += send(ds, cb, S["ac%d" % rank])
+        part_starts()
+        g.wait_ge(S.r_sent, sent)
+    else:
+        part_starts()
+        sent = relay(g, core, rank, relayed(rank, T, topo)[0], T, topo)
+        for i, qs in enumerate(fplane):
+            for q in qs:
+                g.wait_ge(S["ap%d" % q], need[q])
+            sent += send([home], slots(T, slot_of(qs[0], T, topo), len(qs))[1], S["fp%d" % i])
+        for i, qs in enumerate(fcodes):
+            for q in qs:
+                g.wait_ge(S["ac%d" % q], need[q])
+            sent += send([home], slots(T, slot_of(qs[0], T, topo), len(qs))[0].bitcast(dt.uint8), S["fc%d" % i])
+        g.wait_ge(S.qv, 1)
+        sent += copy_to(g, core, [home], T.vp[:, HT:TOK], T.vp[:, 0:HT], S.r_v, S.r_sent, topo)
+        sent += copy_to(g, core, [home], T.vc[:, HT:TOK].bitcast(dt.uint8), T.vc[:, 0:HT].bitcast(dt.uint8), S.r_v, S.r_sent, topo)
+        g.wait_ge(S.r_sent, sent)
+
+    v.memset(T.ones[:], 1.0).then_inc(S.s_ones, 1)
+    if is_rank:
+        v.wait_ge(S.s_tb, 16)
+        v.quantize_mx(c, p, T.tt[:]).then_inc(S.s_qt, 1)
+    v.wait_ge(S.s_hot, 1)
+    for b in range(4):
+        v.quantize_mx(T.ec[:, 128 * b:128 * b + 128], T.ep[:, 128 * b:128 * b + 128], T.hot[:, 3 - b:3 - b + 512]).then_inc(S.s_qe, 1)
+    v.wait_ge(S.s_ids, 128)
+    first = 0 if is_rank else L
+    for t in range(4):
+        v.tensor_copy(T.id4[:, L * t:L * t + L], T.idl[:, first:first + L]).then_inc(S.s_id4, 1)
+    v.wait_ge(S.s_id4, 4)
+    for q in range(N):
+        v.tensor_scalar(T.hx[:, W * q:W * q + W], T.id4[:], HA[q], HB[q], AluOpType.mult, AluOpType.add).then_inc(S.s_hx, 1)
+    v.wait_ge(S.s_hx, N)
+    v.tensor_scalar(T.hc[:], T.hx[:], 5, K - 1, AluOpType.logical_shift_right, AluOpType.bitwise_and).then_inc(S.s_hc, 1)
+    v.wait_ge(S.s_hc, 1)
+    v.wait_ge(S.s_cst, 1)
+    v.tensor_tensor(T.ofs[:], T.hc[:], T.cst[:], AluOpType.add).then_inc(S.s_ofs, 1)
+    v.wait_ge(S.s_ofs, 1)
+    v.tensor_copy(T.off[:], T.ofs[:]).then_inc(S.s_off, 1)
+    if is_rank:
+        v.wait_ge(S.s_w, 16)
+        v.quantize_mx(T.wc[:], T.wp[:], T.wt[:]).then_inc(S.s_qw, 1)
+    v.wait_ge(S.s_off, 1)
+
+    g.tensor.wait_ge(S.s_qe, 4)
+    for u, q in enumerate(order):
+        if q == rank and is_rank:
+            g.tensor.wait_ge(S.s_qt, 1)
+        elif q == rank:
+            g.tensor.wait_ge(S.r_plane, n16)
+            g.tensor.wait_ge(S.r_codes, n16)
+        elif is_rank:
+            g.tensor.wait_ge(S["fp%d" % [q in qs for qs in fplane].index(True)], n16)
+            g.tensor.wait_ge(S["fc%d" % [q in qs for qs in fcodes].index(True)], n16)
+        else:
+            g.tensor.wait_ge(S["ap%d" % q], need[q])
+            g.tensor.wait_ge(S["ac%d" % q], need[q])
+        if u >= 2:
+            g.tensor.wait_ge(S["cu%d" % order[u - 2]], 4)
+        qc, qp = slots(T, slot_of(q, T, topo), 1)
+        for b in range(4):
+            a = 512 * (4 * (u % 2) + b)
+            g.tensor.matmul_mx(T.ps[:, a:a + K], T.ec[:, 128 * b:128 * b + 128], T.ep[:, 128 * b:128 * b + 128],
+                               qc, qp, True, True).then_inc(S["mm%d_%d" % (q, b)], 1)
+
+    def bring(eng, q, bs):
+        for b in bs:
+            eng.wait_ge(S["mm%d_%d" % (q, b)], 1)
+            a = 512 * (4 * (order.index(q) % 2) + b)
+            d = 4 * K * q + K * b
+            if eng is v:
+                v.tensor_copy(T.dd[:, d:d + K], T.ps[:, a:a + K]).then_inc(S["cu%d" % q], 1)
+            else:
+                eng.activation(T.dd[:, d:d + K], T.ps[:, a:a + K], ActivationFunctionType.Copy).then_inc(S["cu%d" % q], 1)
+
+    shared = [order[1], seq[1]]
+    for q in order:
+        bring(g.scalar, q, [0, 1] if q in shared else [0, 1, 2, 3])
+
+    bring(v, order[1], [2, 3])
+    for k, q in enumerate(seq):
+        if k == 1:
+            bring(v, q, [2, 3])
+        win = T.dd[:, 4 * K * q:4 * K * q + 4 * K]
+        v.wait_ge(S["cu%d" % q], 4)
+        if k > 0:
+            v.wait_ge(S["add%d" % (k - 1)], 1)
+        if k == 0:
+            v.tensor_copy(T.acc[:], win.indirect(T.off[:, W * q:W * q + W])).then_inc(S["add%d" % k], 1)
+        elif k < N - 1:
+            v.tensor_tensor(T.acc[:], win.indirect(T.off[:, W * q:W * q + W]), T.acc[:], AluOpType.add).then_inc(S["add%d" % k], 1)
+        else:
+            for t in range(4):
+                v.tensor_tensor(T.vt[:, t:4 * HT:4], win.indirect(T.off[:, W * q + L * t:W * q + L * t + L]),
+                                T.acc[:, HT * t:HT * t + HT], AluOpType.add).then_inc(S.lv, 1)
+    v.wait_ge(S.lv, 4)
+    v.quantize_mx(T.vc[:, 0:HT], T.vp[:, 0:HT], T.vt[:]).then_inc(S.qv, 1)
+
+    if not is_rank:
+        return
+    g.tensor.wait_ge(S.s_qw, 1)
+    g.tensor.wait_ge(S["cu%d" % order[N - 2]], 4)
+    for h in range(2):
+        if h == 0:
+            g.tensor.wait_ge(S.qv, 1)
+        else:
+            g.tensor.wait_ge(S.r_v, 2 * n16)
+        g.tensor.matmul_mx(T.ps[:, 512 * h:512 * h + HT], T.wc[:], T.wp[:], T.vc[:, HT * h:HT * h + HT], T.vp[:, HT * h:HT * h + HT],
+                           True, True).then_inc(S["ym%d" % h], 1)
+    v.wait_ge(S.ym0, 1)
+    v.tensor_copy(T.yt[:, 0:HT], T.ps[:, 0:HT]).then_inc(S.yc0, 1)
+    g.sync.wait_ge(S.yc0, 1)
+    g.sync.dma_start(T.y[:, 0:HT], T.yt[:, 0:HT]).then_inc(S.s_o0, 16)
+    g.scalar.wait_ge(S.ym1, 1)
+    g.scalar.activation(T.yt[:, HT:TOK], T.ps[:, 512:512 + HT], ActivationFunctionType.Copy).then_inc(S.yc1, 1)
+    g.scalar.wait_ge(S.yc1, 1)
+    g.scalar.dma_start(T.y[:, HT:TOK], T.yt[:, HT:TOK]).then_inc(S.s_o1, 16)
+    g.sync.wait_ge(S.s_o0, 16)
+    g.scalar.wait_ge(S.s_o1, 16)

@@ -1,9 +1,10 @@
 from concourse.bass import DstId, RemoteDMATransfer
 from concourse.mybir import dt, AluOpType, ActivationFunctionType
 
-N, TOK, K = 8, 256, 256
+N, TOK, K, WORLD = 8, 256, 256, 256
 HA = (1237, 1811, 947, 1543, 2017, 733, 1409, 1699)
 HB = (40503, 12289, 58111, 3571, 27644, 61007, 19211, 50021)
+LATE = (4, 5, 6, 7)
 HT = TOK // 2
 L = HT // 16
 W = 4 * L
@@ -22,11 +23,19 @@ SCRATCH = {
     "ido": ("dram", [128, TOK // 128], "int32"),
     "idd": ("dram", [128, TOK // 128], "int32"),
     "idl": ("sbuf", [128, TOK // 16], "int32"),
-    "id4": ("sbuf", [128, W], "int32"),
-    "hx": ("sbuf", [128, N * W], "int32"),
-    "hc": ("sbuf", [128, N * W], "int32"),
-    "cst": ("sbuf", [128, N * W], "int32"),
-    "ofs": ("sbuf", [128, N * W], "int32"),
+    "par": ("sbuf", [128, 2 * N], "int32"),
+    "tab": ("sbuf", [128, 2 * N], "int32"),
+    "col": ("sbuf", [128, 2 * N], "int32"),
+    "src": ("sbuf", [128, 2 * N], "int32"),
+    "rp8": ("sbuf", [128, N // 2], "uint16"),
+    "rp4": ("sbuf", [128, 2 * N], "uint16"),
+    "ha": ("sbuf", [128, N * L], "float32"),
+    "hb": ("sbuf", [128, N * L], "float32"),
+    "hm": ("sbuf", [128, N * L], "float32"),
+    "hx": ("sbuf", [128, N * L], "int32"),
+    "hc": ("sbuf", [128, N * L], "int32"),
+    "cst": ("sbuf", [128, N * W], "float32"),
+    "ofs": ("sbuf", [128, N * W], "float32"),
     "off": ("sbuf", [128, N * W], "uint16"),
     "dd": ("sbuf", [128, N * 4 * K], "bfloat16"),
     "acc": ("sbuf", [128, 4 * HT], "float32"),
@@ -36,10 +45,11 @@ SCRATCH = {
     "yt": ("sbuf", [128, TOK], "float32"),
     "ps": ("psum", [128, 8 * 512], "float32"),
 }
-SEMAPHORES = (["s_tb", "s_ido", "s_ids", "s_w", "s_ones", "s_hot", "s_cst", "s_qt", "s_qe", "s_id4", "s_hx", "s_hc", "s_ofs", "s_off",
-               "s_qw", "s_o0", "s_o1", "r_ids", "r_codes", "r_plane", "r_sent", "r_v", "lv", "qv", "ym0", "ym1", "yc0", "yc1"]
+SEMAPHORES = (["s_tb", "s_ido", "s_ids", "s_w", "s_ones", "s_hot", "s_cst", "s_qt", "s_qe", "s_io", "s_ab", "s_col", "s_src", "s_rp",
+               "s_hm", "s_hx", "s_hc", "s_ofs", "s_off", "s_qw", "s_o0", "s_o1", "r_ids", "r_codes", "r_plane", "r_sent", "r_v",
+               "lv", "qv", "ym0", "ym1", "yc0", "yc1"]
               + ["ac%d" % q for q in range(N)] + ["ap%d" % q for q in range(N)] + ["add%d" % k for k in range(N)]
-              + ["fp%d" % i for i in range(3)] + ["fc%d" % i for i in range(5)] + ["cu%d" % q for q in range(N)]
+              + ["fp%d" % i for i in range(5)] + ["fc%d" % i for i in range(7)] + ["cu%d" % q for q in range(N)]
               + ["mm%d_%d" % (q, b) for q in range(N) for b in range(4)])
 
 
@@ -53,29 +63,61 @@ def sides(rank, T, topo):
     return (a, b) if rank in a else (b, a)
 
 
-def relays_of(rank, T, topo):
+def crew(rank, T, topo):
     home = T.cores[rank]
     mine, other = sides(rank, T, topo)
-    owners = [x for x in topo.cores_of(home) if x != home and all(topo.may_write(x, T.cores[d]) for d in other)]
+    rest = [x for x in topo.cores_of(home) if x != home]
+    owners = [x for x in rest if all(topo.may_write(x, T.cores[d]) for d in other)]
     near = [x for x in owners if topo.die(x) == topo.die(home)]
-    far = [x for x in owners if topo.die(x) != topo.die(home)]
-    return near[0], far[0]
+    return near[0], near[1], [x for x in owners if x not in near]
 
 
 def helper(rank, T, topo):
-    return relays_of(rank, T, topo)[0]
+    return crew(rank, T, topo)[0]
 
 
-def direct(rank, T, topo):
+def gates(rank, T, topo):
+    home = T.cores[rank]
+    ms = [x for x in range(WORLD) if topo.mates(home, x) and topo.may_write(x, home)]
+    return [[x for x in ms if (topo.die(x) == topo.die(home)) == near] for near in (True, False)]
+
+
+def landing(q, d, T, topo):
+    if q not in LATE or q == d:
+        return helper(d, T, topo)
+    near, far = gates(d, T, topo)
+    if d in LATE:
+        return (near + far)[[x for x in LATE if x != d].index(q)]
+    return (far if q in sides(d, T, topo)[0] else near)[LATE.index(q) // 2]
+
+
+def senders(rank, T, topo):
     mine, other = sides(rank, T, topo)
     me = mine.index(rank)
-    return [helper(mine[me ^ x], T, topo) for x in (1, 2, 3)]
+    H, near, far = crew(rank, T, topo)
+    same = [landing(rank, d, T, topo) for d in mine]
+    cross = [landing(rank, d, T, topo) for d in other]
+    a, b = me % 2, 1 - me % 2
+    if rank in LATE:
+        by_r, by_h = [cross[a], cross[b]], [same[5 - me]]
+        relays = {far[0]: [same[a], same[b]], far[1]: [cross[2 + a], cross[2 + b]]}
+    else:
+        by_r, by_h = [[same[3], same[1]], [same[0], same[3]]][me], [same[2]]
+        relays = {far[0]: [cross[2 + a], cross[2 + b]], near: [cross[a], cross[b]]}
+    plan = {x: (to, to) for x, to in relays.items()}
+    plan.update({H: (by_r + by_h, by_h), T.cores[rank]: ([], by_r)})
+    return plan
 
 
-def relayed(rank, T, topo):
-    mine, other = sides(rank, T, topo)
-    me = mine.index(rank)
-    return [[helper(other[me ^ x], T, topo) for x in xs] for xs in ((0, 1), (2, 3))]
+def needs(core, T, topo):
+    needp, needc = [0] * N, [0] * N
+    for q in range(N):
+        for src, (to_p, to_c) in senders(q, T, topo).items():
+            if core in to_p:
+                needp[q] += count(common(src, to_p, topo))
+            if core in to_c:
+                needc[q] += count(common(src, to_c, topo))
+    return needp, needc
 
 
 def count(m):
@@ -89,68 +131,62 @@ def common(src, dsts, topo):
     return m
 
 
-def copy_to(g, src, dsts, out, in_, remote_sem, local_sem, topo):
+def write(g, src, dsts, out, in_, remote_sem, T, topo):
     m = common(src, dsts, topo)
-    ids = []
-    for d in dsts:
-        rid, pid = topo.addr(d, src)
-        ids.append(DstId(rid=rid, pnc=pid))
-    g.remote_dma_fused([RemoteDMATransfer(dst_ids=ids, dma_engine_mask=m, remote_sem=remote_sem,
-                                          srcs=[in_], dsts=[out] * len(dsts))], local_sem=local_sem)
+    ids = [DstId(rid=topo.addr(d, src)[0], pnc=topo.addr(d, src)[1]) for d in dsts]
+    g.remote_dma_fused([RemoteDMATransfer(dst_ids=ids, dma_engine_mask=m, remote_sem=remote_sem, srcs=[in_], dsts=[out] * len(dsts))],
+                       local_sem=T.sem.r_sent)
     return count(m)
 
 
-def slot_of(q, T, topo):
-    a, b = planes_of(T, topo)
-    return (a + b).index(q)
+def tables(T, q, n):
+    return T.codes[:, K * q:K * q + K * n], T.planes[:, K * q:K * q + K * n]
 
 
-def slots(T, s, n):
-    return T.codes[:, K * s:K * s + K * n], T.planes[:, K * s:K * s + K * n]
+def hand_on(g, core, q, waits, dsts, T, topo):
+    c, p = tables(T, q, 1)
+    sent = 0
+    for ap, (sem, n), to, kind in zip((p, c.bitcast(dt.uint8)), waits, dsts, "pc"):
+        g.wait_ge(sem, n)
+        sent += write(g, core, to, ap, ap, T.sem["a%s%d" % (kind, q)], T, topo)
+    return sent
 
 
-def relay(g, core, rank, dsts, T, topo):
-    S = T.sem
-    c, p = slots(T, slot_of(rank, T, topo), 1)
+def relay(g, core, rank, T, topo):
     n = count(topo.mask(T.cores[rank], core))
-    g.wait_ge(S.r_plane, n)
-    sent = copy_to(g, core, dsts, p, p, S["ap%d" % rank], S.r_sent, topo)
-    g.wait_ge(S.r_codes, n)
-    return sent + copy_to(g, core, dsts, c.bitcast(dt.uint8), c.bitcast(dt.uint8), S["ac%d" % rank], S.r_sent, topo)
+    return hand_on(g, core, rank, [(T.sem.r_plane, n), (T.sem.r_codes, n)], senders(rank, T, topo)[core], T, topo)
+
+
+def gate(g, core, q, d, T, topo):
+    needp, needc = needs(core, T, topo)
+    H = [helper(d, T, topo)]
+    return hand_on(g, core, q, [(T.sem["ap%d" % q], needp[q]), (T.sem["ac%d" % q], needc[q])], [H, H], T, topo)
 
 
 def rank_program(g, core, T, topo):
-    rank = T.rank_of(core)
-    if rank is not None:
-        lookup_core(g, core, rank, True, T, topo)
-        return
-    for q, home in enumerate(T.cores):
-        if core in topo.cores_of(home):
-            H, F = relays_of(q, T, topo)
-            if core == H:
-                lookup_core(g, core, q, False, T, topo)
-            elif core == F:
-                sent = relay(g, core, q, relayed(q, T, topo)[1], T, topo)
-                g.wait_ge(T.sem.r_sent, sent)
+    for d in range(N):
+        if core in (T.cores[d], helper(d, T, topo)):
+            lookup_core(g, core, d, T, topo)
+        elif core in senders(d, T, topo):
+            g.wait_ge(T.sem.r_sent, relay(g, core, d, T, topo))
+        for q in LATE:
+            if q != d and core == landing(q, d, T, topo) != helper(d, T, topo):
+                g.wait_ge(T.sem.r_sent, gate(g, core, q, d, T, topo))
 
 
-def lookup_core(g, core, rank, is_rank, T, topo):
+def lookup_core(g, core, rank, T, topo):
     S = T.sem
     v = g.vector
     home = T.cores[rank]
-    H, F = relays_of(rank, T, topo)
+    is_rank = core == home
+    H, near, far = crew(rank, T, topo)
     mine, other = sides(rank, T, topo)
-    me = mine.index(rank)
-    o = 2 - 2 * (me // 2)
     n16 = count(topo.mask(H, home))
 
-    need = {}
-    for q in range(N):
-        if q == rank:
-            continue
-        for src, dsts in [(T.cores[q], direct(q, T, topo))] + list(zip(relays_of(q, T, topo), relayed(q, T, topo))):
-            if core in dsts:
-                need[q] = count(common(src, dsts, topo))
+    need = dict(zip("pc", needs(core, T, topo)))
+    for q in LATE:
+        if landing(q, rank, T, topo) != H:
+            need["p"][q] = need["c"][q] = count(topo.mask(landing(q, rank, T, topo), H))
 
     seq = list(range(N))
     if seq[1] in mine:
@@ -158,13 +194,18 @@ def lookup_core(g, core, rank, is_rank, T, topo):
     order = [rank]
     order += [q for q in seq if q in mine and q not in order][:1]
     order += [q for q in seq if q not in order]
-    fplane = [[mine[me ^ 1]], mine[o:o + 2], other]
-    fcodes = [[mine[me ^ 1]], mine[o:o + 2], other[0:1], other[1:2], other[2:4]]
-    fcodes.sort(key=lambda qs: min(order.index(q) for q in qs))
+    low = [q for q in range(N) if q not in LATE]
+    hand = [("p", qs) for qs in ([q for q in low if q < rank], [q for q in low if q > rank])]
+    hand += [("c", [q]) for q in order if q in low and q != rank]
+    for qs in (LATE[0:1], LATE[1:2], LATE[2:4]):
+        hand += [(kind, [q for q in qs if q != rank]) for kind in "pc"]
+    hand = [(kind, qs) for kind, qs in hand if qs]
+    handed = {(kind, q): "f%s%d" % (kind, [k for k, _ in hand[:i]].count(kind)) for i, (kind, qs) in enumerate(hand) for q in qs}
 
     if is_rank:
+        g.sync.dma_start(T.ido[:], T.ids[:]).then_inc(S.s_ido, 16)
         g.sync.dma_start(T.tt[:], T.tb[:]).then_inc(S.s_tb, 16)
-        g.scalar.dma_start(T.ido[:], T.ids[:]).then_inc(S.s_ido, 16)
+        g.scalar.wait_ge(S.s_ido, 16)
     else:
         for eng in (g.sync, g.scalar):
             eng.wait_ge(S.r_ids, n16)
@@ -174,62 +215,77 @@ def lookup_core(g, core, rank, is_rank, T, topo):
     if is_rank:
         g.sync.dma_start(T.wt[:], T.w[:]).then_inc(S.s_w, 16)
 
+    def one_hot():
+        g.wait_ge(S.s_ones, 1)
+        g.affine_select(T.hot[:], T.ones[:], [[-1, 516]], AluOpType.is_equal, 0.0, 3, 4).then_inc(S.s_hot, 1)
+
     def part_starts():
-        g.iota(T.cst[:], [[0, N], [K, 4], [0, L]], 0, 0).then_inc(S.s_cst, 1)
+        g.iota(T.cst[:], [[0, N], [K, 4], [0, L]], 0, 0, allow_small_or_imprecise_dtypes=True).then_inc(S.s_cst, 1)
 
     def send(dsts, ap, sem):
-        return copy_to(g, core, dsts, ap, ap, sem, S.r_sent, topo)
+        return write(g, core, dsts, ap, ap, sem, T, topo)
 
-    g.wait_ge(S.s_ones, 1)
-    g.affine_select(T.hot[:], T.ones[:], [[-1, 516]], AluOpType.is_equal, 0.0, 3, 4).then_inc(S.s_hot, 1)
-    c, p = slots(T, slot_of(rank, T, topo), 1)
-    cb = c.bitcast(dt.uint8)
+    g.iota(T.par[:], [[0, 2 * N]], 0, 1).then_inc(S.s_io, 1)
+    g.iota(T.tab[:], [[L, N], [0, 2]], 0, 0).then_inc(S.s_io, 1)
+    c, p = tables(T, rank, 1)
     if is_rank:
-        ds = direct(rank, T, topo)
         g.wait_ge(S.s_ido, 16)
-        sent = copy_to(g, core, [H], T.idd[:], T.ido[:], S.r_ids, S.r_sent, topo)
+        sent = write(g, core, [H], T.idd[:], T.ido[:], S.r_ids, T, topo)
         g.wait_ge(S.s_qt, 1)
-        sent += send([H, F], p, S.r_plane)
-        sent += send([H, F], cb, S.r_codes)
-        sent += send(ds, p, S["ap%d" % rank])
-        sent += send(ds, cb, S["ac%d" % rank])
+        relays = [x for x in senders(rank, T, topo) if x not in (H, core)]
+        sent += send([H] + relays, p, S.r_plane)
+        sent += send(relays + [H], c.bitcast(dt.uint8), S.r_codes)
+        sent += send(senders(rank, T, topo)[core][1], c.bitcast(dt.uint8), S["ac%d" % rank])
+        one_hot()
         part_starts()
-        g.wait_ge(S.r_sent, sent)
     else:
+        one_hot()
         part_starts()
-        sent = relay(g, core, rank, relayed(rank, T, topo)[0], T, topo)
-        for i, qs in enumerate(fplane):
+        sent = relay(g, core, rank, T, topo)
+        for kind, qs in hand:
             for q in qs:
-                g.wait_ge(S["ap%d" % q], need[q])
-            sent += send([home], slots(T, slot_of(qs[0], T, topo), len(qs))[1], S["fp%d" % i])
-        for i, qs in enumerate(fcodes):
-            for q in qs:
-                g.wait_ge(S["ac%d" % q], need[q])
-            sent += send([home], slots(T, slot_of(qs[0], T, topo), len(qs))[0].bitcast(dt.uint8), S["fc%d" % i])
+                g.wait_ge(S["a%s%d" % (kind, q)], need[kind][q])
+            hc, hp = tables(T, qs[0], len(qs))
+            sent += send([home], hp if kind == "p" else hc.bitcast(dt.uint8), S[handed[kind, qs[0]]])
         g.wait_ge(S.qv, 1)
-        sent += copy_to(g, core, [home], T.vp[:, HT:TOK], T.vp[:, 0:HT], S.r_v, S.r_sent, topo)
-        sent += copy_to(g, core, [home], T.vc[:, HT:TOK].bitcast(dt.uint8), T.vc[:, 0:HT].bitcast(dt.uint8), S.r_v, S.r_sent, topo)
-        g.wait_ge(S.r_sent, sent)
+        sent += send([home], T.vc[:, 0:HT].bitcast(dt.uint8), S.r_v)
+        sent += send([home], T.vp[:, 0:HT], S.r_v)
+    g.wait_ge(S.r_sent, sent)
+
+    def pack_one_hot():
+        v.wait_ge(S.s_hot, 1)
+        for b in range(4):
+            v.quantize_mx(T.ec[:, 128 * b:128 * b + 128], T.ep[:, 128 * b:128 * b + 128], T.hot[:, 3 - b:3 - b + 512]).then_inc(S.s_qe, 1)
 
     v.memset(T.ones[:], 1.0).then_inc(S.s_ones, 1)
     if is_rank:
         v.wait_ge(S.s_tb, 16)
         v.quantize_mx(c, p, T.tt[:]).then_inc(S.s_qt, 1)
-    v.wait_ge(S.s_hot, 1)
-    for b in range(4):
-        v.quantize_mx(T.ec[:, 128 * b:128 * b + 128], T.ep[:, 128 * b:128 * b + 128], T.hot[:, 3 - b:3 - b + 512]).then_inc(S.s_qe, 1)
-    v.wait_ge(S.s_ids, 128)
-    first = 0 if is_rank else L
-    for t in range(4):
-        v.tensor_copy(T.id4[:, L * t:L * t + L], T.idl[:, first:first + L]).then_inc(S.s_id4, 1)
-    v.wait_ge(S.s_id4, 4)
+        pack_one_hot()
     for q in range(N):
-        v.tensor_scalar(T.hx[:, W * q:W * q + W], T.id4[:], HA[q], HB[q], AluOpType.mult, AluOpType.add).then_inc(S.s_hx, 1)
-    v.wait_ge(S.s_hx, N)
+        v.memset(T.ha[:, L * q:L * q + L], float(HA[q])).then_inc(S.s_ab, 1)
+        v.memset(T.hb[:, L * q:L * q + L], float(HB[q])).then_inc(S.s_ab, 1)
+    v.wait_ge(S.s_io, 2)
+    v.tensor_scalar(T.col[:], T.par[:], L - 1, None, AluOpType.bitwise_and).then_inc(S.s_col, 1)
+    v.wait_ge(S.s_col, 1)
+    v.tensor_copy(T.rp8[:], T.col[:, 0:N // 2]).then_inc(S.s_rp, 1)
+    v.tensor_tensor(T.src[:], T.col[:], T.tab[:], AluOpType.add).then_inc(S.s_src, 1)
+    v.wait_ge(S.s_src, 1)
+    v.tensor_copy(T.rp4[:], T.src[:]).then_inc(S.s_rp, 1)
+    if not is_rank:
+        pack_one_hot()
+    v.wait_ge(S.s_rp, 2)
+    v.wait_ge(S.s_ab, 2 * N)
+    v.wait_ge(S.s_ids, 128)
+    first = L if is_rank else 0
+    v.tensor_tensor(T.hm[:], T.idl[:, first:first + L].indirect(T.rp8[:]), T.ha[:], AluOpType.mult).then_inc(S.s_hm, 1)
+    v.wait_ge(S.s_hm, 1)
+    v.tensor_tensor(T.hx[:], T.hm[:], T.hb[:], AluOpType.add).then_inc(S.s_hx, 1)
+    v.wait_ge(S.s_hx, 1)
     v.tensor_scalar(T.hc[:], T.hx[:], 5, K - 1, AluOpType.logical_shift_right, AluOpType.bitwise_and).then_inc(S.s_hc, 1)
     v.wait_ge(S.s_hc, 1)
     v.wait_ge(S.s_cst, 1)
-    v.tensor_tensor(T.ofs[:], T.hc[:], T.cst[:], AluOpType.add).then_inc(S.s_ofs, 1)
+    v.tensor_tensor(T.ofs[:], T.hc[:].indirect(T.rp4[:]), T.cst[:], AluOpType.add).then_inc(S.s_ofs, 1)
     v.wait_ge(S.s_ofs, 1)
     v.tensor_copy(T.off[:], T.ofs[:]).then_inc(S.s_off, 1)
     if is_rank:
@@ -244,17 +300,17 @@ def lookup_core(g, core, rank, is_rank, T, topo):
         elif q == rank:
             g.tensor.wait_ge(S.r_plane, n16)
             g.tensor.wait_ge(S.r_codes, n16)
-        elif is_rank:
-            g.tensor.wait_ge(S["fp%d" % [q in qs for qs in fplane].index(True)], n16)
-            g.tensor.wait_ge(S["fc%d" % [q in qs for qs in fcodes].index(True)], n16)
         else:
-            g.tensor.wait_ge(S["ap%d" % q], need[q])
-            g.tensor.wait_ge(S["ac%d" % q], need[q])
-        if u >= 2:
-            g.tensor.wait_ge(S["cu%d" % order[u - 2]], 4)
-        qc, qp = slots(T, slot_of(q, T, topo), 1)
+            for kind in "pc":
+                if is_rank:
+                    g.tensor.wait_ge(S[handed[kind, q]], n16)
+                else:
+                    g.tensor.wait_ge(S["a%s%d" % (kind, q)], need[kind][q])
+        qc, qp = tables(T, q, 1)
         for b in range(4):
             a = 512 * (4 * (u % 2) + b)
+            if u >= 2:
+                g.tensor.wait_ge(S["cu%d" % (a // 512)], u // 2)
             g.tensor.matmul_mx(T.ps[:, a:a + K], T.ec[:, 128 * b:128 * b + 128], T.ep[:, 128 * b:128 * b + 128],
                                qc, qp, True, True).then_inc(S["mm%d_%d" % (q, b)], 1)
 
@@ -264,20 +320,26 @@ def lookup_core(g, core, rank, is_rank, T, topo):
             a = 512 * (4 * (order.index(q) % 2) + b)
             d = 4 * K * q + K * b
             if eng is v:
-                v.tensor_copy(T.dd[:, d:d + K], T.ps[:, a:a + K]).then_inc(S["cu%d" % q], 1)
+                v.tensor_copy(T.dd[:, d:d + K], T.ps[:, a:a + K]).then_inc(S["cu%d" % (a // 512)], 1)
             else:
-                eng.activation(T.dd[:, d:d + K], T.ps[:, a:a + K], ActivationFunctionType.Copy).then_inc(S["cu%d" % q], 1)
+                eng.activation(T.dd[:, d:d + K], T.ps[:, a:a + K], ActivationFunctionType.Copy).then_inc(S["cu%d" % (a // 512)], 1)
 
-    shared = [order[1], seq[1]]
+    by_v = {q: 0 for q in order}
+    by_v.update({order[1]: 2, seq[1]: 2})
+    by_v.update({order[4]: 1, order[6]: 1})
+    by_v[rank] = 0
     for q in order:
-        bring(g.scalar, q, [0, 1] if q in shared else [0, 1, 2, 3])
+        bring(g.scalar, q, range(4 - by_v[q]))
 
-    bring(v, order[1], [2, 3])
+    brought = 0
     for k, q in enumerate(seq):
-        if k == 1:
-            bring(v, q, [2, 3])
+        ahead = max(order.index(x) for x in seq[:k + (2 if k else 1)])
+        while brought <= ahead:
+            bring(v, order[brought], range(4 - by_v[order[brought]], 4))
+            brought += 1
         win = T.dd[:, 4 * K * q:4 * K * q + 4 * K]
-        v.wait_ge(S["cu%d" % q], 4)
+        for b in range(4):
+            v.wait_ge(S["cu%d" % (4 * (order.index(q) % 2) + b)], order.index(q) // 2 + 1)
         if k > 0:
             v.wait_ge(S["add%d" % (k - 1)], 1)
         if k == 0:
@@ -289,26 +351,25 @@ def lookup_core(g, core, rank, is_rank, T, topo):
                 v.tensor_tensor(T.vt[:, t:4 * HT:4], win.indirect(T.off[:, W * q + L * t:W * q + L * t + L]),
                                 T.acc[:, HT * t:HT * t + HT], AluOpType.add).then_inc(S.lv, 1)
     v.wait_ge(S.lv, 4)
-    v.quantize_mx(T.vc[:, 0:HT], T.vp[:, 0:HT], T.vt[:]).then_inc(S.qv, 1)
+    a = 16 * first
+    v.quantize_mx(T.vc[:, a:a + HT], T.vp[:, a:a + HT], T.vt[:]).then_inc(S.qv, 1)
 
     if not is_rank:
         return
     g.tensor.wait_ge(S.s_qw, 1)
-    g.tensor.wait_ge(S["cu%d" % order[N - 2]], 4)
-    for h in range(2):
-        if h == 0:
-            g.tensor.wait_ge(S.qv, 1)
-        else:
-            g.tensor.wait_ge(S.r_v, 2 * n16)
+    for b in range(2):
+        g.tensor.wait_ge(S["cu%d" % b], N // 2)
+    for h, sem, n in ((1, S.qv, 1), (0, S.r_v, 2 * n16)):
+        g.tensor.wait_ge(sem, n)
         g.tensor.matmul_mx(T.ps[:, 512 * h:512 * h + HT], T.wc[:], T.wp[:], T.vc[:, HT * h:HT * h + HT], T.vp[:, HT * h:HT * h + HT],
                            True, True).then_inc(S["ym%d" % h], 1)
-    v.wait_ge(S.ym0, 1)
-    v.tensor_copy(T.yt[:, 0:HT], T.ps[:, 0:HT]).then_inc(S.yc0, 1)
-    g.sync.wait_ge(S.yc0, 1)
-    g.sync.dma_start(T.y[:, 0:HT], T.yt[:, 0:HT]).then_inc(S.s_o0, 16)
-    g.scalar.wait_ge(S.ym1, 1)
-    g.scalar.activation(T.yt[:, HT:TOK], T.ps[:, 512:512 + HT], ActivationFunctionType.Copy).then_inc(S.yc1, 1)
-    g.scalar.wait_ge(S.yc1, 1)
-    g.scalar.dma_start(T.y[:, HT:TOK], T.yt[:, HT:TOK]).then_inc(S.s_o1, 16)
-    g.sync.wait_ge(S.s_o0, 16)
-    g.scalar.wait_ge(S.s_o1, 16)
+    v.wait_ge(S.ym1, 1)
+    v.tensor_copy(T.yt[:, HT:TOK], T.ps[:, 512:512 + HT]).then_inc(S.yc1, 1)
+    g.sync.wait_ge(S.yc1, 1)
+    g.sync.dma_start(T.y[:, HT:TOK], T.yt[:, HT:TOK]).then_inc(S.s_o1, 16)
+    g.scalar.wait_ge(S.ym0, 1)
+    g.scalar.activation(T.yt[:, 0:HT], T.ps[:, 0:HT], ActivationFunctionType.Copy).then_inc(S.yc0, 1)
+    g.scalar.wait_ge(S.yc0, 1)
+    g.scalar.dma_start(T.y[:, 0:HT], T.yt[:, 0:HT]).then_inc(S.s_o0, 16)
+    g.sync.wait_ge(S.s_o1, 16)
+    g.scalar.wait_ge(S.s_o0, 16)

@@ -48,8 +48,8 @@ SCRATCH = {
 SEMAPHORES = (["s_tb", "s_ido", "s_ids", "s_w", "s_ones", "s_hot", "s_cst", "s_qt", "s_qe", "s_io", "s_ab", "s_col", "s_src", "s_rp",
                "s_hm", "s_hx", "s_hc", "s_ofs", "s_off", "s_qw", "s_o0", "s_o1", "r_ids", "r_codes", "r_plane", "r_sent", "r_v",
                "lv", "qv", "ym0", "ym1", "yc0", "yc1"]
-              + ["ac%d" % q for q in range(N)] + ["ap%d" % q for q in range(N)] + ["add%d" % k for k in range(N)]
-              + ["fp%d" % i for i in range(5)] + ["fc%d" % i for i in range(7)] + ["cu%d" % q for q in range(N)]
+              + ["ac%d" % q for q in range(N)] + ["ap%d" % q for q in range(N)] + ["add0", "add1"]
+              + ["fp%d" % i for i in range(7)] + ["fc%d" % i for i in range(7)] + ["cu%d" % q for q in range(N)]
               + ["mm%d_%d" % (q, b) for q in range(N) for b in range(4)])
 
 
@@ -83,7 +83,7 @@ def gates(rank, T, topo):
 
 
 def landing(q, d, T, topo):
-    if q not in LATE or q == d:
+    if q not in LATE or q == d or (q in LATE[:2] and (d not in LATE or q in sides(d, T, topo)[0])):
         return helper(d, T, topo)
     near, far = gates(d, T, topo)
     if d in LATE:
@@ -101,6 +101,9 @@ def senders(rank, T, topo):
     if rank in LATE:
         by_r, by_h = [cross[a], cross[b]], [same[5 - me]]
         relays = {far[0]: [same[a], same[b]], far[1]: [cross[2 + a], cross[2 + b]]}
+        if rank in LATE[:2]:
+            x = LATE.index(rank)
+            by_r, relays = [cross[3], cross[2]], {far[0]: [same[x], same[1 - x]], far[1]: [cross[x], cross[1 - x]]}
     else:
         by_r, by_h = [[same[3], same[1]], [same[0], same[3]]][me], [same[2]]
         relays = {far[0]: [cross[2 + a], cross[2 + b]], near: [cross[a], cross[b]]}
@@ -189,14 +192,14 @@ def lookup_core(g, core, rank, T, topo):
             need["p"][q] = need["c"][q] = count(topo.mask(landing(q, rank, T, topo), H))
 
     seq = list(range(N))
-    if seq[1] in mine:
+    straight = H in senders(mine[0], T, topo)[T.cores[mine[0]]][1] + senders(mine[1], T, topo)[T.cores[mine[1]]][1]
+    if (seq[1] in mine) == straight:
         seq[0], seq[1] = seq[1], seq[0]
     order = [rank]
-    order += [q for q in seq if q in mine and q not in order][:1]
+    order += [q for q in seq if q in mine and q not in order and straight][:1]
     order += [q for q in seq if q not in order]
     low = [q for q in range(N) if q not in LATE]
-    hand = [("p", qs) for qs in ([q for q in low if q < rank], [q for q in low if q > rank])]
-    hand += [("c", [q]) for q in order if q in low and q != rank]
+    hand = [(kind, [q]) for q in order if q in low and q != rank for kind in "pc"]
     for qs in (LATE[0:1], LATE[1:2], LATE[2:4]):
         hand += [(kind, [q for q in qs if q != rank]) for kind in "pc"]
     hand = [(kind, qs) for kind, qs in hand if qs]
@@ -220,27 +223,26 @@ def lookup_core(g, core, rank, T, topo):
         g.affine_select(T.hot[:], T.ones[:], [[-1, 516]], AluOpType.is_equal, 0.0, 3, 4).then_inc(S.s_hot, 1)
 
     def part_starts():
-        g.iota(T.cst[:], [[0, N], [K, 4], [0, L]], 0, 0, allow_small_or_imprecise_dtypes=True).then_inc(S.s_cst, 1)
+        g.iota(T.cst[:], [[0, 2 * N], [K, 2], [0, L]], 0, 0, allow_small_or_imprecise_dtypes=True).then_inc(S.s_cst, 1)
 
     def send(dsts, ap, sem):
         return write(g, core, dsts, ap, ap, sem, T, topo)
 
     g.iota(T.par[:], [[0, 2 * N]], 0, 1).then_inc(S.s_io, 1)
     g.iota(T.tab[:], [[L, N], [0, 2]], 0, 0).then_inc(S.s_io, 1)
+    part_starts()
     c, p = tables(T, rank, 1)
     if is_rank:
         g.wait_ge(S.s_ido, 16)
         sent = write(g, core, [H], T.idd[:], T.ido[:], S.r_ids, T, topo)
         g.wait_ge(S.s_qt, 1)
         relays = [x for x in senders(rank, T, topo) if x not in (H, core)]
-        sent += send([H] + relays, p, S.r_plane)
+        sent += send(relays[:1] + [H] + relays[1:], p, S.r_plane)
         sent += send(relays + [H], c.bitcast(dt.uint8), S.r_codes)
         sent += send(senders(rank, T, topo)[core][1], c.bitcast(dt.uint8), S["ac%d" % rank])
         one_hot()
-        part_starts()
     else:
         one_hot()
-        part_starts()
         sent = relay(g, core, rank, T, topo)
         for kind, qs in hand:
             for q in qs:
@@ -261,7 +263,6 @@ def lookup_core(g, core, rank, T, topo):
     if is_rank:
         v.wait_ge(S.s_tb, 16)
         v.quantize_mx(c, p, T.tt[:]).then_inc(S.s_qt, 1)
-        pack_one_hot()
     for q in range(N):
         v.memset(T.ha[:, L * q:L * q + L], float(HA[q])).then_inc(S.s_ab, 1)
         v.memset(T.hb[:, L * q:L * q + L], float(HB[q])).then_inc(S.s_ab, 1)
@@ -289,6 +290,7 @@ def lookup_core(g, core, rank, T, topo):
     v.wait_ge(S.s_ofs, 1)
     v.tensor_copy(T.off[:], T.ofs[:]).then_inc(S.s_off, 1)
     if is_rank:
+        pack_one_hot()
         v.wait_ge(S.s_w, 16)
         v.quantize_mx(T.wc[:], T.wp[:], T.wt[:]).then_inc(S.s_qw, 1)
     v.wait_ge(S.s_off, 1)
@@ -328,28 +330,30 @@ def lookup_core(g, core, rank, T, topo):
     by_v.update({order[1]: 2, seq[1]: 2})
     by_v.update({order[4]: 1, order[6]: 1})
     by_v[rank] = 0
+    by_v = {q: range(n) if q == order[1] else range(4 - n, 4) for q, n in by_v.items()}
     for q in order:
-        bring(g.scalar, q, range(4 - by_v[q]))
+        bring(g.scalar, q, [b for b in range(4) if b not in by_v[q]])
 
     brought = 0
     for k, q in enumerate(seq):
         ahead = max(order.index(x) for x in seq[:k + (2 if k else 1)])
         while brought <= ahead:
-            bring(v, order[brought], range(4 - by_v[order[brought]], 4))
+            bring(v, order[brought], by_v[order[brought]])
             brought += 1
-        win = T.dd[:, 4 * K * q:4 * K * q + 4 * K]
-        for b in range(4):
-            v.wait_ge(S["cu%d" % (4 * (order.index(q) % 2) + b)], order.index(q) // 2 + 1)
-        if k > 0:
-            v.wait_ge(S["add%d" % (k - 1)], 1)
-        if k == 0:
-            v.tensor_copy(T.acc[:], win.indirect(T.off[:, W * q:W * q + W])).then_inc(S["add%d" % k], 1)
-        elif k < N - 1:
-            v.tensor_tensor(T.acc[:], win.indirect(T.off[:, W * q:W * q + W]), T.acc[:], AluOpType.add).then_inc(S["add%d" % k], 1)
-        else:
-            for t in range(4):
-                v.tensor_tensor(T.vt[:, t:4 * HT:4], win.indirect(T.off[:, W * q + L * t:W * q + L * t + L]),
-                                T.acc[:, HT * t:HT * t + HT], AluOpType.add).then_inc(S.lv, 1)
+        for ts in ([0, 1], [2, 3]) if k < N - 1 else ([0], [1], [2], [3]):
+            h = ts[0] // 2
+            for b in ts:
+                v.wait_ge(S["cu%d" % (4 * (order.index(q) % 2) + b)], order.index(q) // 2 + 1)
+            if k > 0:
+                v.wait_ge(S["add%d" % h], k)
+            win = T.dd[:, 4 * K * q + 2 * K * h:4 * K * q + K * (ts[-1] + 1)].indirect(T.off[:, W * q + L * ts[0]:W * q + L * (ts[-1] + 1)])
+            acc = T.acc[:, HT * ts[0]:HT * (ts[-1] + 1)]
+            if k == 0:
+                v.tensor_copy(acc, win).then_inc(S["add%d" % h], 1)
+            elif k < N - 1:
+                v.tensor_tensor(acc, win, acc, AluOpType.add).then_inc(S["add%d" % h], 1)
+            else:
+                v.tensor_tensor(T.vt[:, ts[0]:4 * HT:4], win, acc, AluOpType.add).then_inc(S.lv, 1)
     v.wait_ge(S.lv, 4)
     a = 16 * first
     v.quantize_mx(T.vc[:, a:a + HT], T.vp[:, a:a + HT], T.vt[:]).then_inc(S.qv, 1)

from concourse.bass import DstId, RemoteDMATransfer
from concourse.mybir import dt, AluOpType, ActivationFunctionType

N, TOK, K, WORLD = 8, 256, 256, 256
HA = (1237, 1811, 947, 1543, 2017, 733, 1409, 1699)
HB = (40503, 12289, 58111, 3571, 27644, 61007, 19211, 50021)
LATE = (4, 5, 6, 7)
HT = TOK // 2
L = HT // 16
W = 4 * L

SCRATCH = {
    "codes": ("sbuf", [128, N * K], "float8_e4m3fn_x4"),
    "planes": ("sbuf", [128, N * K], "uint8"),
    "tt": ("sbuf", [128, 4 * K], "bfloat16"),
    "wt": ("sbuf", [128, 512], "bfloat16"),
    "wc": ("sbuf", [128, 128], "float8_e4m3fn_x4"),
    "wp": ("sbuf", [128, 128], "uint8"),
    "ones": ("sbuf", [128, 516], "bfloat16"),
    "hot": ("sbuf", [128, 516], "bfloat16"),
    "ec": ("sbuf", [128, 512], "float8_e4m3fn_x4"),
    "ep": ("sbuf", [128, 512], "uint8"),
    "ido": ("dram", [128, TOK // 128], "int32"),
    "idd": ("dram", [128, TOK // 128], "int32"),
    "idl": ("sbuf", [128, TOK // 16], "int32"),
    "par": ("sbuf", [128, 2 * N], "int32"),
    "tab": ("sbuf", [128, 2 * N], "int32"),
    "col": ("sbuf", [128, 2 * N], "int32"),
    "src": ("sbuf", [128, 2 * N], "int32"),
    "rp8": ("sbuf", [128, N // 2], "uint16"),
    "rp4": ("sbuf", [128, 2 * N], "uint16"),
    "ha": ("sbuf", [128, N * L], "float32"),
    "hb": ("sbuf", [128, N * L], "float32"),
    "hm": ("sbuf", [128, N * L], "float32"),
    "hx": ("sbuf", [128, N * L], "int32"),
    "hc": ("sbuf", [128, N * L], "int32"),
    "cst": ("sbuf", [128, N * W], "float32"),
    "ofs": ("sbuf", [128, N * W], "float32"),
    "off": ("sbuf", [128, N * W], "uint16"),
    "dd": ("sbuf", [128, N * 4 * K], "bfloat16"),
    "acc": ("sbuf", [128, 4 * HT], "float32"),
    "vt": ("sbuf", [128, 4 * HT], "bfloat16"),
    "vc": ("sbuf", [128, TOK], "float8_e4m3fn_x4"),
    "vp": ("sbuf", [128, TOK], "uint8"),
    "yt": ("sbuf", [128, TOK], "float32"),
    "ps": ("psum", [128, 8 * 512], "float32"),
}
SEMAPHORES = (["s_tb", "s_ido", "s_ids", "s_w", "s_ones", "s_hot", "s_cst", "s_qt", "s_qe", "s_io", "s_ab", "s_col", "s_src", "s_rp",
               "s_hm", "s_hx", "s_hc", "s_ofs", "s_off", "s_qw", "s_o0", "s_o1", "r_ids", "r_codes", "r_plane", "r_sent", "r_v",
               "lv", "qv", "ym0", "ym1", "yc0", "yc1"]
              + ["ac%d" % q for q in range(N)] + ["ap%d" % q for q in range(N)] + ["add0", "add1"]
              + ["fp%d" % i for i in range(7)] + ["fc%d" % i for i in range(7)] + ["cu%d" % q for q in range(N)]
              + ["mm%d_%d" % (q, b) for q in range(N) for b in range(4)])


def planes_of(T, topo):
    a = [q for q in range(N) if q == 0 or topo.same_plane(T.cores[0], T.cores[q])]
    return a, [q for q in range(N) if q not in a]


def sides(rank, T, topo):
    a, b = planes_of(T, topo)
    return (a, b) if rank in a else (b, a)


def crew(rank, T, topo):
    home = T.cores[rank]
    mine, other = sides(rank, T, topo)
    rest = [x for x in topo.cores_of(home) if x != home]
    owners = [x for x in rest if all(topo.may_write(x, T.cores[d]) for d in other)]
    near = [x for x in owners if topo.die(x) == topo.die(home)]
    return near[0], near[1], [x for x in owners if x not in near]


def helper(rank, T, topo):
    return crew(rank, T, topo)[0]


def gates(rank, T, topo):
    home = T.cores[rank]
    ms = [x for x in range(WORLD) if topo.mates(home, x) and topo.may_write(x, home)]
    return [[x for x in ms if (topo.die(x) == topo.die(home)) == near] for near in (True, False)]


def landing(q, d, T, topo):
    if q not in LATE or q == d or (q in LATE[:2] and (d not in LATE or q in sides(d, T, topo)[0])):
        return helper(d, T, topo)
    near, far = gates(d, T, topo)
    if d in LATE:
        return (near + far)[[x for x in LATE if x != d].index(q)]
    return (far if q in sides(d, T, topo)[0] else near)[LATE.index(q) // 2]


def senders(rank, T, topo):
    mine, other = sides(rank, T, topo)
    me = mine.index(rank)
    H, near, far = crew(rank, T, topo)
    same = [landing(rank, d, T, topo) for d in mine]
    cross = [landing(rank, d, T, topo) for d in other]
    a, b = me % 2, 1 - me % 2
    if rank in LATE:
        by_r, by_h = [cross[a], cross[b]], [same[5 - me]]
        relays = {far[0]: [same[a], same[b]], far[1]: [cross[2 + a], cross[2 + b]]}
        if rank in LATE[:2]:
            x = LATE.index(rank)
            by_r, relays = [cross[3], cross[2]], {far[0]: [same[x], same[1 - x]], far[1]: [cross[x], cross[1 - x]]}
    else:
        by_r, by_h = [[same[3], same[1]], [same[0], same[3]]][me], [same[2]]
        relays = {far[0]: [cross[2 + a], cross[2 + b]], near: [cross[a], cross[b]]}
    plan = {x: (to, to) for x, to in relays.items()}
    plan.update({H: (by_r + by_h, by_h), T.cores[rank]: ([], by_r)})
    return plan


def needs(core, T, topo):
    needp, needc = [0] * N, [0] * N
    for q in range(N):
        for src, (to_p, to_c) in senders(q, T, topo).items():
            if core in to_p:
                needp[q] += count(common(src, to_p, topo))
            if core in to_c:
                needc[q] += count(common(src, to_c, topo))
    return needp, needc


def count(m):
    return bin(m).count("1")


def common(src, dsts, topo):
    m = topo.mask(src, dsts[0])
    for d in dsts:
        m &= topo.mask(src, d)
    return m


def write(g, src, dsts, out, in_, remote_sem, T, topo):
    m = common(src, dsts, topo)
    ids = [DstId(rid=topo.addr(d, src)[0], pnc=topo.addr(d, src)[1]) for d in dsts]
    g.remote_dma_fused([RemoteDMATransfer(dst_ids=ids, dma_engine_mask=m, remote_sem=remote_sem, srcs=[in_], dsts=[out] * len(dsts))],
                       local_sem=T.sem.r_sent)
    return count(m)


def tables(T, q, n):
    return T.codes[:, K * q:K * q + K * n], T.planes[:, K * q:K * q + K * n]


def hand_on(g, core, q, waits, dsts, T, topo):
    c, p = tables(T, q, 1)
    sent = 0
    for ap, (sem, n), to, kind in zip((p, c.bitcast(dt.uint8)), waits, dsts, "pc"):
        g.wait_ge(sem, n)
        sent += write(g, core, to, ap, ap, T.sem["a%s%d" % (kind, q)], T, topo)
    return sent


def relay(g, core, rank, T, topo):
    n = count(topo.mask(T.cores[rank], core))
    return hand_on(g, core, rank, [(T.sem.r_plane, n), (T.sem.r_codes, n)], senders(rank, T, topo)[core], T, topo)


def gate(g, core, q, d, T, topo):
    needp, needc = needs(core, T, topo)
    H = [helper(d, T, topo)]
    return hand_on(g, core, q, [(T.sem["ap%d" % q], needp[q]), (T.sem["ac%d" % q], needc[q])], [H, H], T, topo)


def rank_program(g, core, T, topo):
    for d in range(N):
        if core in (T.cores[d], helper(d, T, topo)):
            lookup_core(g, core, d, T, topo)
        elif core in senders(d, T, topo):
            g.wait_ge(T.sem.r_sent, relay(g, core, d, T, topo))
        for q in LATE:
            if q != d and core == landing(q, d, T, topo) != helper(d, T, topo):
                g.wait_ge(T.sem.r_sent, gate(g, core, q, d, T, topo))


def lookup_core(g, core, rank, T, topo):
    S = T.sem
    v = g.vector
    home = T.cores[rank]
    is_rank = core == home
    H, near, far = crew(rank, T, topo)
    mine, other = sides(rank, T, topo)
    n16 = count(topo.mask(H, home))

    need = dict(zip("pc", needs(core, T, topo)))
    for q in LATE:
        if landing(q, rank, T, topo) != H:
            need["p"][q] = need["c"][q] = count(topo.mask(landing(q, rank, T, topo), H))

    seq = list(range(N))
    straight = H in senders(mine[0], T, topo)[T.cores[mine[0]]][1] + senders(mine[1], T, topo)[T.cores[mine[1]]][1]
    if (seq[1] in mine) == straight:
        seq[0], seq[1] = seq[1], seq[0]
    order = [rank]
    order += [q for q in seq if q in mine and q not in order and straight][:1]
    order += [q for q in seq if q not in order]
    low = [q for q in range(N) if q not in LATE]
    hand = [(kind, [q]) for q in order if q in low and q != rank for kind in "pc"]
    for qs in (LATE[0:1], LATE[1:2], LATE[2:4]):
        hand += [(kind, [q for q in qs if q != rank]) for kind in "pc"]
    hand = [(kind, qs) for kind, qs in hand if qs]
    handed = {(kind, q): "f%s%d" % (kind, [k for k, _ in hand[:i]].count(kind)) for i, (kind, qs) in enumerate(hand) for q in qs}

    if is_rank:
        g.sync.dma_start(T.ido[:], T.ids[:]).then_inc(S.s_ido, 16)
        g.sync.dma_start(T.tt[:], T.tb[:]).then_inc(S.s_tb, 16)
        g.scalar.wait_ge(S.s_ido, 16)
    else:
        for eng in (g.sync, g.scalar):
            eng.wait_ge(S.r_ids, n16)
    for k in range(8):
        eng = g.scalar if k % 2 == 0 else g.sync
        eng.dma_start(T.idl[16 * k:16 * k + 16, :], T.ids[:] if is_rank else T.idd[:]).then_inc(S.s_ids, 16)
    if is_rank:
        g.sync.dma_start(T.wt[:], T.w[:]).then_inc(S.s_w, 16)

    def one_hot():
        g.wait_ge(S.s_ones, 1)
        g.affine_select(T.hot[:], T.ones[:], [[-1, 516]], AluOpType.is_equal, 0.0, 3, 4).then_inc(S.s_hot, 1)

    def part_starts():
        g.iota(T.cst[:], [[0, 2 * N], [K, 2], [0, L]], 0, 0, allow_small_or_imprecise_dtypes=True).then_inc(S.s_cst, 1)

    def send(dsts, ap, sem):
        return write(g, core, dsts, ap, ap, sem, T, topo)

    g.iota(T.par[:], [[0, 2 * N]], 0, 1).then_inc(S.s_io, 1)
    g.iota(T.tab[:], [[L, N], [0, 2]], 0, 0).then_inc(S.s_io, 1)
    part_starts()
    c, p = tables(T, rank, 1)
    if is_rank:
        g.wait_ge(S.s_ido, 16)
        sent = write(g, core, [H], T.idd[:], T.ido[:], S.r_ids, T, topo)
        g.wait_ge(S.s_qt, 1)
        relays = [x for x in senders(rank, T, topo) if x not in (H, core)]
        sent += send(relays[:1] + [H] + relays[1:], p, S.r_plane)
        sent += send(relays + [H], c.bitcast(dt.uint8), S.r_codes)
        sent += send(senders(rank, T, topo)[core][1], c.bitcast(dt.uint8), S["ac%d" % rank])
        one_hot()
    else:
        one_hot()
        sent = relay(g, core, rank, T, topo)
        for kind, qs in hand:
            for q in qs:
                g.wait_ge(S["a%s%d" % (kind, q)], need[kind][q])
            hc, hp = tables(T, qs[0], len(qs))
            sent += send([home], hp if kind == "p" else hc.bitcast(dt.uint8), S[handed[kind, qs[0]]])
        g.wait_ge(S.qv, 1)
        sent += send([home], T.vc[:, 0:HT].bitcast(dt.uint8), S.r_v)
        sent += send([home], T.vp[:, 0:HT], S.r_v)
    g.wait_ge(S.r_sent, sent)

    def pack_one_hot():
        v.wait_ge(S.s_hot, 1)
        for b in range(4):
            v.quantize_mx(T.ec[:, 128 * b:128 * b + 128], T.ep[:, 128 * b:128 * b + 128], T.hot[:, 3 - b:3 - b + 512]).then_inc(S.s_qe, 1)

    v.memset(T.ones[:], 1.0).then_inc(S.s_ones, 1)
    if is_rank:
        v.wait_ge(S.s_tb, 16)
        v.quantize_mx(c, p, T.tt[:]).then_inc(S.s_qt, 1)
    for q in range(N):
        v.memset(T.ha[:, L * q:L * q + L], float(HA[q])).then_inc(S.s_ab, 1)
        v.memset(T.hb[:, L * q:L * q + L], float(HB[q])).then_inc(S.s_ab, 1)
    v.wait_ge(S.s_io, 2)
    v.tensor_scalar(T.col[:], T.par[:], L - 1, None, AluOpType.bitwise_and).then_inc(S.s_col, 1)
    v.wait_ge(S.s_col, 1)
    v.tensor_copy(T.rp8[:], T.col[:, 0:N // 2]).then_inc(S.s_rp, 1)
    v.tensor_tensor(T.src[:], T.col[:], T.tab[:], AluOpType.add).then_inc(S.s_src, 1)
    v.wait_ge(S.s_src, 1)
    v.tensor_copy(T.rp4[:], T.src[:]).then_inc(S.s_rp, 1)
    if not is_rank:
        pack_one_hot()
    v.wait_ge(S.s_rp, 2)
    v.wait_ge(S.s_ab, 2 * N)
    v.wait_ge(S.s_ids, 128)
    first = L if is_rank else 0
    v.tensor_tensor(T.hm[:], T.idl[:, first:first + L].indirect(T.rp8[:]), T.ha[:], AluOpType.mult).then_inc(S.s_hm, 1)
    v.wait_ge(S.s_hm, 1)
    v.tensor_tensor(T.hx[:], T.hm[:], T.hb[:], AluOpType.add).then_inc(S.s_hx, 1)
    v.wait_ge(S.s_hx, 1)
    v.tensor_scalar(T.hc[:], T.hx[:], 5, K - 1, AluOpType.logical_shift_right, AluOpType.bitwise_and).then_inc(S.s_hc, 1)
    v.wait_ge(S.s_hc, 1)
    v.wait_ge(S.s_cst, 1)
    v.tensor_tensor(T.ofs[:], T.hc[:].indirect(T.rp4[:]), T.cst[:], AluOpType.add).then_inc(S.s_ofs, 1)
    v.wait_ge(S.s_ofs, 1)
    v.tensor_copy(T.off[:], T.ofs[:]).then_inc(S.s_off, 1)
    if is_rank:
        pack_one_hot()
        v.wait_ge(S.s_w, 16)
        v.quantize_mx(T.wc[:], T.wp[:], T.wt[:]).then_inc(S.s_qw, 1)
    v.wait_ge(S.s_off, 1)

    g.tensor.wait_ge(S.s_qe, 4)
    for u, q in enumerate(order):
        if q == rank and is_rank:
            g.tensor.wait_ge(S.s_qt, 1)
        elif q == rank:
            g.tensor.wait_ge(S.r_plane, n16)
            g.tensor.wait_ge(S.r_codes, n16)
        else:
            for kind in "pc":
                if is_rank:
                    g.tensor.wait_ge(S[handed[kind, q]], n16)
                else:
                    g.tensor.wait_ge(S["a%s%d" % (kind, q)], need[kind][q])
        qc, qp = tables(T, q, 1)
        for b in range(4):
            a = 512 * (4 * (u % 2) + b)
            if u >= 2:
                g.tensor.wait_ge(S["cu%d" % (a // 512)], u // 2)
            g.tensor.matmul_mx(T.ps[:, a:a + K], T.ec[:, 128 * b:128 * b + 128], T.ep[:, 128 * b:128 * b + 128],
                               qc, qp, True, True).then_inc(S["mm%d_%d" % (q, b)], 1)

    def bring(eng, q, bs):
        for b in bs:
            eng.wait_ge(S["mm%d_%d" % (q, b)], 1)
            a = 512 * (4 * (order.index(q) % 2) + b)
            d = 4 * K * q + K * b
            if eng is v:
                v.tensor_copy(T.dd[:, d:d + K], T.ps[:, a:a + K]).then_inc(S["cu%d" % (a // 512)], 1)
            else:
                eng.activation(T.dd[:, d:d + K], T.ps[:, a:a + K], ActivationFunctionType.Copy).then_inc(S["cu%d" % (a // 512)], 1)

    by_v = {q: 0 for q in order}
    by_v.update({order[1]: 2, seq[1]: 2})
    by_v.update({order[4]: 1, order[6]: 1})
    by_v[rank] = 0
    by_v = {q: range(n) if q == order[1] else range(4 - n, 4) for q, n in by_v.items()}
    for q in order:
        bring(g.scalar, q, [b for b in range(4) if b not in by_v[q]])

    brought = 0
    for k, q in enumerate(seq):
        ahead = max(order.index(x) for x in seq[:k + (2 if k else 1)])
        while brought <= ahead:
            bring(v, order[brought], by_v[order[brought]])
            brought += 1
        for ts in ([0, 1], [2, 3]) if k < N - 1 else ([0], [1], [2], [3]):
            h = ts[0] // 2
            for b in ts:
                v.wait_ge(S["cu%d" % (4 * (order.index(q) % 2) + b)], order.index(q) // 2 + 1)
            if k > 0:
                v.wait_ge(S["add%d" % h], k)
            win = T.dd[:, 4 * K * q + 2 * K * h:4 * K * q + K * (ts[-1] + 1)].indirect(T.off[:, W * q + L * ts[0]:W * q + L * (ts[-1] + 1)])
            acc = T.acc[:, HT * ts[0]:HT * (ts[-1] + 1)]
            if k == 0:
                v.tensor_copy(acc, win).then_inc(S["add%d" % h], 1)
            elif k < N - 1:
                v.tensor_tensor(acc, win, acc, AluOpType.add).then_inc(S["add%d" % h], 1)
            else:
                v.tensor_tensor(T.vt[:, ts[0]:4 * HT:4], win, acc, AluOpType.add).then_inc(S.lv, 1)
    v.wait_ge(S.lv, 4)
    a = 16 * first
    v.quantize_mx(T.vc[:, a:a + HT], T.vp[:, a:a + HT], T.vt[:]).then_inc(S.qv, 1)

    if not is_rank:
        return
    g.tensor.wait_ge(S.s_qw, 1)
    for b in range(2):
        g.tensor.wait_ge(S["cu%d" % b], N // 2)
    for h, sem, n in ((1, S.qv, 1), (0, S.r_v, 2 * n16)):
        g.tensor.wait_ge(sem, n)
        g.tensor.matmul_mx(T.ps[:, 512 * h:512 * h + HT], T.wc[:], T.wp[:], T.vc[:, HT * h:HT * h + HT], T.vp[:, HT * h:HT * h + HT],
                           True, True).then_inc(S["ym%d" % h], 1)
    v.wait_ge(S.ym1, 1)
    v.tensor_copy(T.yt[:, HT:TOK], T.ps[:, 512:512 + HT]).then_inc(S.yc1, 1)
    g.sync.wait_ge(S.yc1, 1)
    g.sync.dma_start(T.y[:, HT:TOK], T.yt[:, HT:TOK]).then_inc(S.s_o1, 16)
    g.scalar.wait_ge(S.ym0, 1)
    g.scalar.activation(T.yt[:, 0:HT], T.ps[:, 0:HT], ActivationFunctionType.Copy).then_inc(S.yc0, 1)
    g.scalar.wait_ge(S.yc0, 1)
    g.scalar.dma_start(T.y[:, 0:HT], T.yt[:, 0:HT]).then_inc(S.s_o0, 16)
    g.sync.wait_ge(S.s_o1, 16)
    g.scalar.wait_ge(S.s_o0, 16)
